import numpy as np
import ml_dtypes

BF16 = ml_dtypes.bfloat16


def bf(x):
    return np.asarray(x, np.float32).astype(BF16)


def f32(x):
    return np.asarray(x, np.float32)


def f64(x):
    return np.asarray(x).astype(np.float64)


def striped(idx):
    return np.tile(idx.reshape(-1, 16).T, (8, 1))


S, K, M, N, V, D = 256, 128, 128, 256, 128, 2


def sigmoid(v):
    return 1.0 / (1.0 + np.exp(-v))


def setup_inputs():
    return {"table": bf(np.random.standard_normal((K, S))), "w": bf(np.random.standard_normal((D, K, M)) / np.sqrt(K)), "b": f32(0.5 * np.random.standard_normal((M, 1))), "offs": striped(np.random.permutation(np.tile(np.arange(S), 2))[:N])}


def reference(table, w, b, offs):
    idx = offs[:16].T.reshape(-1)
    x = f64(table)[:, idx]
    p = f64(w)[0].T @ x[:, :V]
    q = f64(w)[1].T @ x[:, V:]
    return p * sigmoid(q + f64(b))

@@ -1,0 +1,44 @@
+import concourse.mybir as mybir
+
+NODES, FEATURES, OUT_FEATURES, EDGES = 256, 128, 128, 128
+HALVES = 2
+SOURCE, TARGET = 0, 1
+ENTRIES_PER_COLUMN = 16
+HALF_COLUMNS = EDGES // ENTRIES_PER_COLUMN
+
+FLOPS = 2 * HALVES * FEATURES * OUT_FEATURES * EDGES
+
+BF16, F32, U16 = mybir.dt.bfloat16, mybir.dt.float32, mybir.dt.uint16
+SIGMOID = mybir.ActivationFunctionType.Sigmoid
+MULT = mybir.AluOpType.mult
+
+
+def tile_rows_pair_gate_rep_kernel(tc, table, w, b, offs, out):
+    nc = tc.nc
+    with (
+        tc.tile_pool(name="held", bufs=1) as held,
+        tc.psum_pool(name="psum", bufs=1) as psum,
+    ):
+        nodes = held.tile([FEATURES, NODES], BF16, name="nodes")
+        offsets = held.tile([FEATURES, HALVES * HALF_COLUMNS], U16, name="offsets")
+        weights = held.tile([FEATURES, HALVES, OUT_FEATURES], BF16, name="weights")
+        bias = held.tile([OUT_FEATURES, 1], F32, name="bias")
+        nc.sync.dma_start(nodes[:], table)
+        nc.sync.dma_start(offsets[:], offs)
+        nc.scalar.dma_start(weights[:], w.rearrange("d k m -> k d m"))
+        nc.scalar.dma_start(bias[:], b)
+
+        def project(half, name):
+            product = psum.tile([OUT_FEATURES, EDGES], F32, name=name)
+            half_list = offsets[:, half * HALF_COLUMNS : (half + 1) * HALF_COLUMNS]
+            nc.tensor.matmul(product[:], weights[:, half, :], nodes[:].indirect(half_list), start=True, stop=True)
+            return product
+
+        q = project(TARGET, "q")
+        p = project(SOURCE, "p")
+
+        gate = held.tile([OUT_FEATURES, EDGES], F32, name="gate")
+        nc.scalar.activation(gate[:], q[:], SIGMOID, bias=bias[:])
+        message = held.tile([OUT_FEATURES, EDGES], F32, name="message")
+        nc.vector.tensor_tensor(message[:], p[:], gate[:], MULT)
+        nc.sync.dma_start(out, message[:])

@@ -28,6 +28,11 @@ def tile_rows_pair_gate_rep_kernel(tc, table, w, b, offs, out):
         nc.scalar.dma_start(weights[:], w.rearrange("d k m -> k d m"))
         nc.scalar.dma_start(bias[:], b)
 
+        warm_in = held.tile([OUT_FEATURES, 1], F32, name="warm_in")
+        warm_out = held.tile([OUT_FEATURES, 1], F32, name="warm_out")
+        nc.vector.memset(warm_in[:], 0.0)
+        nc.scalar.activation(warm_out[:], warm_in[:], SIGMOID)
+
         def project(half, name):
             product = psum.tile([OUT_FEATURES, EDGES], F32, name=name)
             half_list = offsets[:, half * HALF_COLUMNS : (half + 1) * HALF_COLUMNS]

@@ -21,12 +21,13 @@ def tile_rows_pair_gate_rep_kernel(tc, table, w, b, offs, out):
     ):
         nodes = held.tile([FEATURES, NODES], BF16, name="nodes")
         offsets = held.tile([FEATURES, HALVES * HALF_COLUMNS], U16, name="offsets")
-        weights = held.tile([FEATURES, HALVES, OUT_FEATURES], BF16, name="weights")
+        weights = [held.tile([FEATURES, OUT_FEATURES], BF16, name=f"weights{half}") for half in range(HALVES)]
         bias = held.tile([OUT_FEATURES, 1], F32, name="bias")
         nc.sync.dma_start(nodes[:], table)
         nc.sync.dma_start(offsets[:], offs)
-        nc.scalar.dma_start(weights[:], w.rearrange("d k m -> k d m"))
+        nc.scalar.dma_start(weights[TARGET][:], w[TARGET])
         nc.scalar.dma_start(bias[:], b)
+        nc.sync.dma_start(weights[SOURCE][:], w[SOURCE])
 
         warm_in = held.tile([OUT_FEATURES, 1], F32, name="warm_in")
         warm_out = held.tile([OUT_FEATURES, 1], F32, name="warm_out")
@@ -36,7 +37,7 @@ def tile_rows_pair_gate_rep_kernel(tc, table, w, b, offs, out):
         def project(half, name):
             product = psum.tile([OUT_FEATURES, EDGES], F32, name=name)
             half_list = offsets[:, half * HALF_COLUMNS : (half + 1) * HALF_COLUMNS]
-            nc.tensor.matmul(product[:], weights[:, half, :], nodes[:].indirect(half_list), start=True, stop=True)
+            nc.tensor.matmul(product[:], weights[half][:], nodes[:].indirect(half_list), start=True, stop=True)
             return product
 
         q = project(TARGET, "q")

import concourse.mybir as mybir

NODES, FEATURES, OUT_FEATURES, EDGES = 256, 128, 128, 128
HALVES = 2
SOURCE, TARGET = 0, 1
ENTRIES_PER_COLUMN = 16
HALF_COLUMNS = EDGES // ENTRIES_PER_COLUMN

FLOPS = 2 * HALVES * FEATURES * OUT_FEATURES * EDGES

BF16, F32, U16 = mybir.dt.bfloat16, mybir.dt.float32, mybir.dt.uint16
SIGMOID = mybir.ActivationFunctionType.Sigmoid
MULT = mybir.AluOpType.mult


def tile_rows_pair_gate_rep_kernel(tc, table, w, b, offs, out):
    nc = tc.nc
    with (
        tc.tile_pool(name="held", bufs=1) as held,
        tc.psum_pool(name="psum", bufs=1) as psum,
    ):
        nodes = held.tile([FEATURES, NODES], BF16, name="nodes")
        offsets = held.tile([FEATURES, HALVES * HALF_COLUMNS], U16, name="offsets")
        weights = [held.tile([FEATURES, OUT_FEATURES], BF16, name=f"weights{half}") for half in range(HALVES)]
        bias = held.tile([OUT_FEATURES, 1], F32, name="bias")
        nc.sync.dma_start(nodes[:], table)
        nc.sync.dma_start(offsets[:], offs)
        nc.scalar.dma_start(weights[TARGET][:], w[TARGET])
        nc.scalar.dma_start(bias[:], b)
        nc.sync.dma_start(weights[SOURCE][:], w[SOURCE])

        warm_in = held.tile([OUT_FEATURES, 1], F32, name="warm_in")
        warm_out = held.tile([OUT_FEATURES, 1], F32, name="warm_out")
        nc.vector.memset(warm_in[:], 0.0)
        nc.scalar.activation(warm_out[:], warm_in[:], SIGMOID)

        def project(half, name):
            product = psum.tile([OUT_FEATURES, EDGES], F32, name=name)
            half_list = offsets[:, half * HALF_COLUMNS : (half + 1) * HALF_COLUMNS]
            nc.tensor.matmul(product[:], weights[half][:], nodes[:].indirect(half_list), start=True, stop=True)
            return product

        q = project(TARGET, "q")
        p = project(SOURCE, "p")

        gate = held.tile([OUT_FEATURES, EDGES], F32, name="gate")
        nc.scalar.activation(gate[:], q[:], SIGMOID, bias=bias[:])
        message = held.tile([OUT_FEATURES, EDGES], F32, name="message")
        nc.vector.tensor_tensor(message[:], p[:], gate[:], MULT)
        nc.sync.dma_start(out, message[:])
